import numpy as np
import ml_dtypes


def mxq(x, axis, fmt="e4m3"):
    dtype, down = {"e4m3": (ml_dtypes.float8_e4m3fn, 7), "e5m2": (ml_dtypes.float8_e5m2, 14)}[fmt]
    v = np.moveaxis(np.asarray(x, np.float32).astype(ml_dtypes.bfloat16).astype(np.float64), axis, -1)
    blocks = v.reshape(v.shape[:-1] + (-1, 32))
    amax = np.abs(blocks).max(-1, keepdims=True)
    byte = np.maximum(np.where(amax > 0, np.frexp(amax)[1] - 1 + 127, 0) - down, 1)
    scale = np.exp2(byte - 127.0)
    codes = (blocks / scale).astype(np.float32).astype(dtype).astype(np.float64)
    return np.moveaxis((codes * scale).reshape(v.shape), -1, axis)


WIDE = False


def mx_kscale(k):
    if not WIDE:
        return np.ones(k)
    levels = np.array([30, -30])
    if k % 512:
        return np.exp2(np.random.permutation(np.resize(levels, k // 32))).repeat(32)
    a = np.empty((k // 512, 16))
    for p in range(k // 512):
        a[p, :8] = np.random.permutation(np.resize(levels, 8))
        for g in range(8):
            far = levels[np.abs(levels - a[p, g]) >= 10]
            a[p, g + 8] = far[np.random.randint(len(far))]
    return np.exp2(a.ravel()).repeat(32)


def f64(x):
    return np.asarray(x).astype(np.float64)


def striped(idx):
    return np.tile(np.asarray(idx).reshape(-1, 16).T, (8, 1)).astype(np.uint16)


def unstriped(offs):
    return offs[:16].T.reshape(-1).astype(np.int64)


E2M1 = np.array([0.0, 0.5, 1.0, 1.5, 2.0, 3.0, 4.0, 6.0, -0.0, -0.5, -1.0, -1.5, -2.0, -3.0, -4.0, -6.0])


def pack_weight(w, fmt):
    k, n = w.shape
    w = f64(np.asarray(w, np.float32).astype(ml_dtypes.bfloat16)).reshape(k // 32, 32, n)
    amax = np.abs(w).max(1)
    if fmt in ("e4m3", "e5m2"):
        byte = np.frexp(amax)[1] - 1 + 127 - (7 if fmt == "e4m3" else 14)
    else:
        mant, ex = np.frexp(amax / 6.0)
        byte = np.where(mant > 0.5, ex, ex - 1) + 127
    byte = np.clip(np.where(amax > 0, byte, 1), 1, 254)
    scaled = (w * np.exp2(127.0 - byte)[:, None, :]).reshape(k, n).astype(np.float32)
    by_word = np.ascontiguousarray(scaled.reshape(k // 512, 128, 4, n).transpose(0, 1, 3, 2))
    if fmt in ("e4m3", "e5m2"):
        words = by_word.astype(ml_dtypes.float8_e4m3fn if fmt == "e4m3" else ml_dtypes.float8_e5m2).view(np.uint8)
    else:
        c = by_word.astype(ml_dtypes.float4_e2m1fn).view(np.uint8) & 0xF
        words = (c[..., 0::2] | (c[..., 1::2] << 4)).reshape(k // 512, 128, 2 * n)
    return np.ascontiguousarray(words), np.ascontiguousarray(byte.astype(np.uint8).reshape(k // 512, 16, n))


def unpack_weight(words, scales, fmt):
    g, _, n = scales.shape
    words = np.ascontiguousarray(words).reshape(g, 128, n, -1)
    if fmt in ("e4m3", "e5m2"):
        vals = words.view(ml_dtypes.float8_e4m3fn if fmt == "e4m3" else ml_dtypes.float8_e5m2).astype(np.float64)
    else:
        nib = np.empty((g, 128, n, 4), np.uint8)
        nib[..., 0::2] = words & 0xF
        nib[..., 1::2] = words >> 4
        vals = E2M1[nib]
    vals = vals * np.repeat(np.exp2(scales.astype(np.float64) - 127.0), 8, axis=1)[..., None]
    return vals.transpose(0, 1, 3, 2).reshape(g * 512, n)


def sgn(shape):
    return np.random.uniform(0.5, 2.0, shape) * np.where(np.random.standard_normal(shape) < 0, -1.0, 1.0)


K, T, Z, J, R, N, U, E = 512, 1024, 1024, 256, 512, 256, 128, 512


def setup_inputs():
    n = np.random.standard_normal
    idx = np.random.permutation(T)[:J]
    idx2 = np.random.permutation(Z)[:J]
    idx3 = np.random.permutation(J)[:J]
    idx4 = np.random.permutation(J)[:J]
    idx5 = np.random.permutation(J)[:U]
    idx6 = np.random.permutation(E)[:U]
    fk = mx_kscale(K)
    fr = mx_kscale(R)
    xtp = pack_weight(n((K, T)) / fk[:, None], "e2m1")
    xop = pack_weight(n((K, Z)) / fk[:, None], "e5m2")
    wp = pack_weight(n((K, R)) * 1 / np.sqrt(K) * fk[:, None] * fr, "e5m2")
    w2p = pack_weight(n((K, R)) * 1 / np.sqrt(K) * fk[:, None] * fr, "e4m3")
    wbp = pack_weight(n((R, N)) * 1 / np.sqrt(R) / fr[:, None], "e4m3")
    return {
        "xt_words": xtp[0],
        "xt_scales": xtp[1],
        "xo_words": xop[0],
        "xo_scales": xop[1],
        "w_words": wp[0],
        "w_scales": wp[1],
        "w2_words": w2p[0],
        "w2_scales": w2p[1],
        "sa": (np.random.uniform(0.5, 1.6, (R, 1))).astype(np.float32),
        "wb_words": wbp[0],
        "wb_scales": wbp[1],
        "so": (sgn((N, 1))).astype(np.float32),
        "offs": striped(idx),
        "offs2": striped(idx2),
        "offs3": striped(idx3),
        "offs4": striped(idx4),
        "offs5": striped(idx5),
        "offs6": striped(idx6),
    }


def reference(xt_words, xt_scales, xo_words, xo_scales, w_words, w_scales, w2_words, w2_scales, sa, wb_words, wb_scales, so, offs, offs2, offs3, offs4, offs5, offs6):
    idx = unstriped(offs)
    idx2 = unstriped(offs2)
    idx3 = unstriped(offs3)
    idx4 = unstriped(offs4)
    idx5 = unstriped(offs5)
    idx6 = unstriped(offs6)
    xtu = unpack_weight(xt_words, xt_scales, "e2m1")
    xou = unpack_weight(xo_words, xo_scales, "e5m2")
    wu = unpack_weight(w_words, w_scales, "e5m2")
    w2u = unpack_weight(w2_words, w2_scales, "e4m3")
    wbu = unpack_weight(wb_words, wb_scales, "e4m3")
    xtidxg = xtu[:, idx]
    xoidx2g = xou[:, idx2]
    a = wu.T @ xtidxg + w2u.T @ xoidx2g
    b = w2u.T @ xtidxg + wu.T @ xoidx2g
    hid = np.maximum(np.abs(a[:, idx3] * f64(sa) - a[:, idx4]), b)
    hidq = mxq(hid, 0, "e5m2")
    p = wbu.T @ hidq
    m0 = p[:, idx5] * f64(so)
    y = np.zeros((N, E))
    y[:, idx6] = m0
    return y

@@ -1,0 +1,194 @@
+from contextlib import ExitStack
+
+import concourse.mybir as mybir
+
+K, T, Z, J, R, N, U, E = 512, 1024, 1024, 256, 512, 256, 128, 512
+FLOPS = 2 * K * R * J * 4 + 2 * R * N * J
+
+F32 = mybir.dt.float32
+BF16 = mybir.dt.bfloat16
+I32 = mybir.dt.int32
+U32 = mybir.dt.uint32
+U16 = mybir.dt.uint16
+U8 = mybir.dt.uint8
+E4M3 = mybir.dt.float8_e4m3fn_x4
+E5M2 = mybir.dt.float8_e5m2_x4
+E2M1 = mybir.dt.float4_e2m1fn_x4
+ALU = mybir.AluOpType
+ACT = mybir.ActivationFunctionType
+
+P = 128
+PACK = 4
+HALF = J // 2
+
+
+def tile_list_betweenweighed_crossed_one_postedout_kernel(
+    tc, xt_words, xt_scales, xo_words, xo_scales, w_words, w_scales, w2_words, w2_scales, sa,
+    wb_words, wb_scales, so, offs, offs2, offs3, offs4, offs5, offs6, out,
+):
+    nc = tc.nc
+    with ExitStack() as ctx:
+        pool = ctx.enter_context(tc.tile_pool(name="pool", bufs=1))
+        psum = ctx.enter_context(tc.psum_pool(name="psum", bufs=1))
+
+        def sb(name, shape, dtype):
+            return pool.tile(shape, dtype, name=name, align_bytes=64)
+
+        def load_list(name, src):
+            dst = pool.tile(list(src.shape), U16, name=name)
+            nc.sync.dma_start(dst[:], src)
+            return dst
+
+        def load_words(name, src, width, dtype):
+            dst = sb(name, [P, width], dtype)
+            nc.scalar.dma_start(dst[:].bitcast(I32), src.bitcast(I32))
+            return dst
+
+        def load_scale_rows(dst, src):
+            rows = src[0].bitcast(I32).rearrange("(h q r) c -> q r h c", h=2, q=2)
+            for q in range(2):
+                nc.sync.dma_start(dst[32 * q : 32 * q + 4], rows[q])
+
+        xt_s = sb("xt_s", [P, T], U8)
+        xo_rows = sb("xo_rows", [64, 2, Z], U8)
+        ww_s = sb("ww_s", [P, 2, 2, R], U8)
+        wb_s = sb("wb_s", [P, N], U8)
+        nc.vector.memset(xt_s[:].bitcast(I32), 0)
+        nc.vector.memset(xo_rows[:].bitcast(I32), 0)
+        nc.vector.memset(ww_s[0:64].bitcast(I32), 0)
+        nc.vector.memset(wb_s[:].bitcast(I32), 0)
+
+        idx = load_list("idx", offs)
+        xt_w = load_words("xt_w", xt_words[0], T, U16)
+        xt_rows = sb("xt_rows", [4, 4, T], U8)
+        nc.sync.dma_start(xt_rows[:].bitcast(I32), xt_scales[0].bitcast(I32).rearrange("(q r) c -> r q c", r=4))
+        w_raw = load_words("w_raw", w_words[0].rearrange("p c t -> p (c t)"), R, U32)
+        idx2 = load_list("idx2", offs2)
+        w2_raw = load_words("w2_raw", w2_words[0].rearrange("p c t -> p (c t)"), R, U32)
+        idx3 = load_list("idx3", offs3)
+        xo_w = load_words("xo_w", xo_words[0].rearrange("p c t -> p (c t)"), Z, U32)
+        load_scale_rows(xo_rows[:].bitcast(I32), xo_scales)
+        load_scale_rows(ww_s[:].bitcast(I32)[:, :, 0, :], w_scales)
+        load_scale_rows(ww_s[:].bitcast(I32)[:, :, 1, :], w2_scales)
+        idx4 = load_list("idx4", offs4)
+        sa_t = sb("sa_t", [P, PACK], F32)
+        nc.sync.dma_start(sa_t[:], sa.rearrange("(p t) o -> p (t o)", t=PACK))
+        wb_w = sb("wb_w", [P, N], U32)
+        nc.sync.dma_start(wb_w[:].bitcast(I32), wb_words[0].rearrange("p c t -> p (c t)").bitcast(I32))
+        for q in range(4):
+            nc.sync.dma_start(wb_s[32 * q : 32 * q + 4].bitcast(I32), wb_scales[0, 4 * q : 4 * q + 4].bitcast(I32))
+        so_t = sb("so_t", [P, 2], F32)
+        with nc.allow_non_contiguous_dma(reason="one value of so a partition and output tile"):
+            nc.sync.dma_start(so_t[:], so.rearrange("(n p) o -> p (n o)", p=P))
+        idx5 = load_list("idx5", offs5)
+        idx6 = load_list("idx6", offs6)
+
+        xtg_s = sb("xtg_s", [P, J], U8)
+        xtg_w = sb("xtg_w", [P, J], U16)
+        xog_s = sb("xog_s", [P, J], U8)
+        xog_w = sb("xog_w", [P, J], U32)
+        xo_s = sb("xo_s", [P, Z], U8)
+        for q in range(4):
+            nc.vector.tensor_copy(xt_s[32 * q : 32 * q + 4].bitcast(I32), xt_rows[:, q, :].bitcast(I32))
+        nc.vector.tensor_copy(xtg_w[:], xt_w[:].indirect(idx[:]))
+        nc.vector.tensor_copy(xtg_s[:], xt_s[:].indirect(idx[:]))
+        for h in range(2):
+            nc.vector.tensor_copy(xo_s[64 * h : 64 * h + 64].bitcast(I32), xo_rows[:, h, :].bitcast(I32))
+
+        w_w = sb("w_w", [P, PACK, P], U32)
+        w2_w = sb("w2_w", [P, PACK, P], U32)
+        ww_p = sb("ww_p", [P, 2, PACK, P], U8)
+        for dst, src in ((w_w, w_raw), (w2_w, w2_raw)):
+            nc.scalar.copy(
+                dst[:].rearrange("p t (c i) -> p c t i", i=4),
+                src[:].rearrange("p (c i t) -> p c t i", i=4, t=PACK),
+            )
+
+        def deal_scales(which):
+            view = ww_s[:].bitcast(I32)
+            nc.vector.tensor_copy(view[64:128, 0, which], view[0:64, 1, which])
+            nc.vector.tensor_copy(ww_p[:, which], ww_s[:, 0, which].rearrange("p (m t) -> p t m", t=PACK))
+
+        nc.vector.tensor_copy(xog_s[:], xo_s[:].indirect(idx2[:]))
+        deal_scales(0)
+        nc.vector.tensor_copy(xog_w[:], xo_w[:].indirect(idx2[:]))
+        deal_scales(1)
+
+        def product(acc, which, t, token, cols, start, stop):
+            words, fmt = ((w_w, E5M2), (w2_w, E4M3))[which]
+            x_w, x_s, x_fmt = (xtg_w, xtg_s, E2M1) if token else (xog_w, xog_s, E5M2)
+            nc.tensor.matmul_mx(
+                out=acc, lhsT=words[:, t, :].bitcast(fmt), lhsT_scale=ww_p[:, which, t, :],
+                rhs=x_w[:, cols].bitcast(x_fmt), rhs_scale=x_s[:, cols], start=start, stop=stop,
+            )
+
+        a_ps = [psum.tile([P, J], F32, name="a_ps%d" % t, tag="bank%d" % t) for t in range(PACK)]
+        b_ps = [psum.tile([P, PACK, HALF], F32, name="b_ps%d" % h) for h in range(2)]
+        for t in range(PACK):
+            product(a_ps[t][:], 0, t, True, slice(0, J), True, False)
+            product(a_ps[t][:], 1, t, False, slice(0, J), False, True)
+        for h in range(2):
+            cols = slice(h * HALF, (h + 1) * HALF)
+            for t in range(PACK):
+                product(b_ps[h][:, t, :], 1, t, True, cols, True, False)
+                product(b_ps[h][:, t, :], 0, t, False, cols, False, True)
+
+        pages = [sb("page%d" % n, [P, E], F32) for n in range(2)]
+        a_sb = [sb("a_sb%d" % t, [P, J], F32) for t in range(PACK)]
+        scaled = [sb("scaled%d" % h, [P, PACK, HALF], F32) for h in range(2)]
+        diff = [sb("diff%d" % h, [P, PACK, HALF], F32) for h in range(2)]
+        mag = [sb("mag%d" % h, [P, PACK, HALF], F32) for h in range(2)]
+        nc.scalar.copy(a_sb[0][:], a_ps[0][:])
+        for t in range(1, PACK):
+            nc.vector.tensor_copy(a_sb[t][:], a_ps[t][:])
+        for h in range(2):
+            for t in range(PACK):
+                nc.scalar.activation(
+                    scaled[h][:, t, :], a_sb[t][:].indirect(idx3[:, 8 * h : 8 * h + 8]), ACT.Copy, scale=sa_t[:, t : t + 1]
+                )
+        for h in range(2):
+            for t in range(PACK):
+                nc.vector.tensor_tensor(
+                    diff[h][:, t, :], a_sb[t][:].indirect(idx4[:, 8 * h : 8 * h + 8]), scaled[h][:, t, :], ALU.subtract
+                )
+            for pair in range(2):
+                nc.scalar.activation(mag[h][:, 2 * pair : 2 * pair + 2, :], diff[h][:, 2 * pair : 2 * pair + 2, :], ACT.Abs)
+
+        hid = [sb("hid%d" % h, [P, HALF, PACK], BF16) for h in range(2)]
+        hid_w = [sb("hid_w%d" % h, [P, HALF], U32) for h in range(2)]
+        hid_s = [sb("hid_s%d" % h, [P, HALF], U8) for h in range(2)]
+        for h in range(2):
+            nc.vector.tensor_tensor(
+                hid[h][:].rearrange("p (c i) t -> p c t i", i=4),
+                mag[h][:].rearrange("p t (c i) -> p c t i", i=4),
+                b_ps[h][:].rearrange("p t (c i) -> p c t i", i=4),
+                ALU.max,
+            )
+        for h in range(2):
+            nc.vector.quantize_mx(
+                out=hid_w[h][:].bitcast(E5M2), scales=hid_s[h][:], in_=hid[h][:].rearrange("p j t -> p (j t)")
+            )
+
+        p_sb = [sb("p_sb%d" % n, [P, J], F32) for n in range(2)]
+        for h in range(2):
+            for n in range(2):
+                p_ps = psum.tile([P, HALF], F32, name="p_ps%d%d" % (h, n), tag="bank%d" % (2 * h + n))
+                nc.tensor.matmul_mx(
+                    out=p_ps[:], lhsT=wb_w[:, n * P : (n + 1) * P].bitcast(E4M3), lhsT_scale=wb_s[:, n * P : (n + 1) * P],
+                    rhs=hid_w[h][:].bitcast(E5M2), rhs_scale=hid_s[h][:], start=True, stop=True,
+                )
+                dst = p_sb[n][:, h * HALF : (h + 1) * HALF]
+                if h == 1 and n == 0:
+                    nc.vector.tensor_copy(dst, p_ps[:])
+                else:
+                    nc.scalar.copy(dst, p_ps[:])
+
+        for n in range(2):
+            nc.vector.memset(pages[n][:], 0.0)
+        ends = [sb("ends%d" % n, [P, U], F32) for n in range(2)]
+        for n in range(2):
+            nc.scalar.activation(ends[n][:], p_sb[n][:].indirect(idx5[:]), ACT.Copy, scale=so_t[:, n : n + 1])
+        nc.vector.tensor_copy(pages[0][:].indirect(idx6[:]), ends[0][:])
+        nc.scalar.activation(pages[1][:].indirect(idx6[:]), ends[1][:], ACT.Copy)
+        nc.sync.dma_start(out[0:P, :], pages[0][:])
+        nc.scalar.dma_start(out[P : 2 * P, :], pages[1][:])

@@ -19,7 +19,14 @@ ACT = mybir.ActivationFunctionType
 
 P = 128
 PACK = 4
-HALF = J // 2
+QUAD = 32
+LIVE = 4
+HALF_P = P // 2
+HALVES = 2
+HALF = J // HALVES
+HALF_COLS = HALF // 16
+N_TILES = N // P
+W, W2 = 0, 1
 
 
 def tile_list_betweenweighed_crossed_one_postedout_kernel(
@@ -41,152 +48,156 @@ def tile_list_betweenweighed_crossed_one_postedout_kernel(
 
         def load_words(name, src, width, dtype):
             dst = sb(name, [P, width], dtype)
-            nc.scalar.dma_start(dst[:].bitcast(I32), src.bitcast(I32))
+            nc.sync.dma_start(dst[:].bitcast(I32), src.bitcast(I32))
             return dst
 
-        def load_scale_rows(dst, src):
-            rows = src[0].bitcast(I32).rearrange("(h q r) c -> q r h c", h=2, q=2)
-            for q in range(2):
-                nc.sync.dma_start(dst[32 * q : 32 * q + 4], rows[q])
+        def load_scale_rows(queues, dst, src):
+            rows = src[0].bitcast(I32).rearrange("(u q row) c -> q row u c", u=2, q=2)
+            for q, queue in enumerate(queues):
+                queue.dma_start(dst[QUAD * q : QUAD * q + LIVE], rows[q])
 
-        xt_s = sb("xt_s", [P, T], U8)
-        xo_rows = sb("xo_rows", [64, 2, Z], U8)
+        xt_rows = sb("xt_rows", [HALF_P, 2, T], U8)
+        xo_rows = sb("xo_rows", [HALF_P, 2, Z], U8)
         ww_s = sb("ww_s", [P, 2, 2, R], U8)
         wb_s = sb("wb_s", [P, N], U8)
-        nc.vector.memset(xt_s[:].bitcast(I32), 0)
+        ww_view = ww_s[:].bitcast(I32)
+        nc.vector.memset(xt_rows[:].bitcast(I32), 0)
         nc.vector.memset(xo_rows[:].bitcast(I32), 0)
-        nc.vector.memset(ww_s[0:64].bitcast(I32), 0)
+        nc.vector.memset(ww_view[HALF_P:P], 0)
         nc.vector.memset(wb_s[:].bitcast(I32), 0)
 
         idx = load_list("idx", offs)
         xt_w = load_words("xt_w", xt_words[0], T, U16)
-        xt_rows = sb("xt_rows", [4, 4, T], U8)
-        nc.sync.dma_start(xt_rows[:].bitcast(I32), xt_scales[0].bitcast(I32).rearrange("(q r) c -> r q c", r=4))
-        w_raw = load_words("w_raw", w_words[0].rearrange("p c t -> p (c t)"), R, U32)
         idx2 = load_list("idx2", offs2)
+        load_scale_rows((nc.scalar, nc.sync), xt_rows[:].bitcast(I32), xt_scales)
+        load_scale_rows((nc.sync, nc.sync), xo_rows[:].bitcast(I32), xo_scales)
+        w_raw = load_words("w_raw", w_words[0].rearrange("p c t -> p (c t)"), R, U32)
+        xo_w = load_words("xo_w", xo_words[0].rearrange("p c t -> p (c t)"), Z, U32)
+        load_scale_rows((nc.sync, nc.sync), ww_view[HALF_P:P, :, W, :], w_scales)
+        load_scale_rows((nc.sync, nc.sync), ww_view[HALF_P:P, :, W2, :], w2_scales)
         w2_raw = load_words("w2_raw", w2_words[0].rearrange("p c t -> p (c t)"), R, U32)
         idx3 = load_list("idx3", offs3)
-        xo_w = load_words("xo_w", xo_words[0].rearrange("p c t -> p (c t)"), Z, U32)
-        load_scale_rows(xo_rows[:].bitcast(I32), xo_scales)
-        load_scale_rows(ww_s[:].bitcast(I32)[:, :, 0, :], w_scales)
-        load_scale_rows(ww_s[:].bitcast(I32)[:, :, 1, :], w2_scales)
-        idx4 = load_list("idx4", offs4)
         sa_t = sb("sa_t", [P, PACK], F32)
         nc.sync.dma_start(sa_t[:], sa.rearrange("(p t) o -> p (t o)", t=PACK))
-        wb_w = sb("wb_w", [P, N], U32)
-        nc.sync.dma_start(wb_w[:].bitcast(I32), wb_words[0].rearrange("p c t -> p (c t)").bitcast(I32))
-        for q in range(4):
-            nc.sync.dma_start(wb_s[32 * q : 32 * q + 4].bitcast(I32), wb_scales[0, 4 * q : 4 * q + 4].bitcast(I32))
-        so_t = sb("so_t", [P, 2], F32)
+        idx4 = load_list("idx4", offs4)
+        idx5 = load_list("idx5", offs5)
+        wb_w = load_words("wb_w", wb_words[0].rearrange("p c t -> p (c t)"), N, U32)
+        for q in range(P // QUAD):
+            nc.sync.dma_start(
+                wb_s[QUAD * q : QUAD * q + LIVE].bitcast(I32), wb_scales[0, LIVE * q : LIVE * q + LIVE].bitcast(I32)
+            )
+        so_t = sb("so_t", [P, N_TILES], F32)
         with nc.allow_non_contiguous_dma(reason="one value of so a partition and output tile"):
             nc.sync.dma_start(so_t[:], so.rearrange("(n p) o -> p (n o)", p=P))
-        idx5 = load_list("idx5", offs5)
         idx6 = load_list("idx6", offs6)
 
         xtg_s = sb("xtg_s", [P, J], U8)
         xtg_w = sb("xtg_w", [P, J], U16)
         xog_s = sb("xog_s", [P, J], U8)
         xog_w = sb("xog_w", [P, J], U32)
+        xt_s = sb("xt_s", [P, T], U8)
         xo_s = sb("xo_s", [P, Z], U8)
-        for q in range(4):
-            nc.vector.tensor_copy(xt_s[32 * q : 32 * q + 4].bitcast(I32), xt_rows[:, q, :].bitcast(I32))
         nc.vector.tensor_copy(xtg_w[:], xt_w[:].indirect(idx[:]))
+        for u in range(2):
+            for plane, rows in ((xt_s, xt_rows), (xo_s, xo_rows)):
+                nc.vector.tensor_copy(plane[HALF_P * u : HALF_P * (u + 1)].bitcast(I32), rows[:, u, :].bitcast(I32))
         nc.vector.tensor_copy(xtg_s[:], xt_s[:].indirect(idx[:]))
-        for h in range(2):
-            nc.vector.tensor_copy(xo_s[64 * h : 64 * h + 64].bitcast(I32), xo_rows[:, h, :].bitcast(I32))
 
         w_w = sb("w_w", [P, PACK, P], U32)
         w2_w = sb("w2_w", [P, PACK, P], U32)
-        ww_p = sb("ww_p", [P, 2, PACK, P], U8)
+        ww_p = sb("ww_p", [P, PACK, 2, P], U8)
         for dst, src in ((w_w, w_raw), (w2_w, w2_raw)):
             nc.scalar.copy(
-                dst[:].rearrange("p t (c i) -> p c t i", i=4),
-                src[:].rearrange("p (c i t) -> p c t i", i=4, t=PACK),
+                dst[:].rearrange("p (e f) (c i) -> p c e i f", i=4, f=2),
+                src[:].rearrange("p (c i e f) -> p c e i f", i=4, e=2, f=2),
             )
 
-        def deal_scales(which):
-            view = ww_s[:].bitcast(I32)
-            nc.vector.tensor_copy(view[64:128, 0, which], view[0:64, 1, which])
-            nc.vector.tensor_copy(ww_p[:, which], ww_s[:, 0, which].rearrange("p (m t) -> p t m", t=PACK))
-
         nc.vector.tensor_copy(xog_s[:], xo_s[:].indirect(idx2[:]))
-        deal_scales(0)
         nc.vector.tensor_copy(xog_w[:], xo_w[:].indirect(idx2[:]))
-        deal_scales(1)
+        nc.vector.tensor_copy(ww_view[0:HALF_P, 1], ww_view[HALF_P:P, 0])
+        for t in range(PACK):
+            nc.vector.tensor_copy(ww_p[:, t], ww_s[:, 1].rearrange("p s (m t) -> p t s m", t=PACK)[:, t])
 
-        def product(acc, which, t, token, cols, start, stop):
-            words, fmt = ((w_w, E5M2), (w2_w, E4M3))[which]
-            x_w, x_s, x_fmt = (xtg_w, xtg_s, E2M1) if token else (xog_w, xog_s, E5M2)
+        matrices = {W: (w_w, E5M2), W2: (w2_w, E4M3)}
+        tokens = (xtg_w, xtg_s, E2M1)
+        notes = (xog_w, xog_s, E5M2)
+
+        def product(acc, matrix, t, table, cols, start, stop):
+            words, fmt = matrices[matrix]
+            x_w, x_s, x_fmt = table
             nc.tensor.matmul_mx(
-                out=acc, lhsT=words[:, t, :].bitcast(fmt), lhsT_scale=ww_p[:, which, t, :],
+                out=acc, lhsT=words[:, t, :].bitcast(fmt), lhsT_scale=ww_p[:, t, matrix, :],
                 rhs=x_w[:, cols].bitcast(x_fmt), rhs_scale=x_s[:, cols], start=start, stop=stop,
             )
 
         a_ps = [psum.tile([P, J], F32, name="a_ps%d" % t, tag="bank%d" % t) for t in range(PACK)]
-        b_ps = [psum.tile([P, PACK, HALF], F32, name="b_ps%d" % h) for h in range(2)]
+        b_ps = [psum.tile([P, PACK, HALF], F32, name="b_ps%d" % h) for h in range(HALVES)]
         for t in range(PACK):
-            product(a_ps[t][:], 0, t, True, slice(0, J), True, False)
-            product(a_ps[t][:], 1, t, False, slice(0, J), False, True)
-        for h in range(2):
+            product(a_ps[t][:], W, t, tokens, slice(0, J), True, False)
+            product(a_ps[t][:], W2, t, notes, slice(0, J), False, True)
+        for h in range(HALVES):
             cols = slice(h * HALF, (h + 1) * HALF)
             for t in range(PACK):
-                product(b_ps[h][:, t, :], 1, t, True, cols, True, False)
-                product(b_ps[h][:, t, :], 0, t, False, cols, False, True)
+                product(b_ps[h][:, t, :], W2, t, tokens, cols, True, False)
+                product(b_ps[h][:, t, :], W, t, notes, cols, False, True)
 
-        pages = [sb("page%d" % n, [P, E], F32) for n in range(2)]
+        pages = [sb("page%d" % n, [P, E], F32) for n in range(N_TILES)]
         a_sb = [sb("a_sb%d" % t, [P, J], F32) for t in range(PACK)]
-        scaled = [sb("scaled%d" % h, [P, PACK, HALF], F32) for h in range(2)]
-        diff = [sb("diff%d" % h, [P, PACK, HALF], F32) for h in range(2)]
-        mag = [sb("mag%d" % h, [P, PACK, HALF], F32) for h in range(2)]
+        scaled = [sb("scaled%d" % h, [P, PACK, HALF], F32) for h in range(HALVES)]
+        diff = [sb("diff%d" % h, [P, PACK, HALF], F32) for h in range(HALVES)]
+        mag = [sb("mag%d" % h, [P, PACK, HALF], F32) for h in range(HALVES)]
         nc.scalar.copy(a_sb[0][:], a_ps[0][:])
         for t in range(1, PACK):
             nc.vector.tensor_copy(a_sb[t][:], a_ps[t][:])
-        for h in range(2):
+        for h in range(HALVES):
+            entries = slice(HALF_COLS * h, HALF_COLS * (h + 1))
             for t in range(PACK):
                 nc.scalar.activation(
-                    scaled[h][:, t, :], a_sb[t][:].indirect(idx3[:, 8 * h : 8 * h + 8]), ACT.Copy, scale=sa_t[:, t : t + 1]
+                    scaled[h][:, t, :], a_sb[t][:].indirect(idx3[:, entries]), ACT.Copy, scale=sa_t[:, t : t + 1]
                 )
-        for h in range(2):
+        for h in range(HALVES):
+            entries = slice(HALF_COLS * h, HALF_COLS * (h + 1))
             for t in range(PACK):
                 nc.vector.tensor_tensor(
-                    diff[h][:, t, :], a_sb[t][:].indirect(idx4[:, 8 * h : 8 * h + 8]), scaled[h][:, t, :], ALU.subtract
+                    diff[h][:, t, :], a_sb[t][:].indirect(idx4[:, entries]), scaled[h][:, t, :], ALU.subtract
                 )
-            for pair in range(2):
-                nc.scalar.activation(mag[h][:, 2 * pair : 2 * pair + 2, :], diff[h][:, 2 * pair : 2 * pair + 2, :], ACT.Abs)
+            for tiles in (slice(0, PACK - 1), slice(PACK - 1, PACK)):
+                nc.scalar.activation(mag[h][:, tiles, :], diff[h][:, tiles, :], ACT.Abs)
 
-        hid = [sb("hid%d" % h, [P, HALF, PACK], BF16) for h in range(2)]
-        hid_w = [sb("hid_w%d" % h, [P, HALF], U32) for h in range(2)]
-        hid_s = [sb("hid_s%d" % h, [P, HALF], U8) for h in range(2)]
-        for h in range(2):
+        hid = [sb("hid%d" % h, [P, HALF, PACK], BF16) for h in range(HALVES)]
+        hid_w = [sb("hid_w%d" % h, [P, HALF], U32) for h in range(HALVES)]
+        hid_s = [sb("hid_s%d" % h, [P, HALF], U8) for h in range(HALVES)]
+        for h in range(HALVES):
             nc.vector.tensor_tensor(
-                hid[h][:].rearrange("p (c i) t -> p c t i", i=4),
-                mag[h][:].rearrange("p t (c i) -> p c t i", i=4),
-                b_ps[h][:].rearrange("p t (c i) -> p c t i", i=4),
+                hid[h][:].rearrange("p (c i) t -> p c t i", i=2),
+                mag[h][:].rearrange("p t (c i) -> p c t i", i=2),
+                b_ps[h][:].rearrange("p t (c i) -> p c t i", i=2),
                 ALU.max,
             )
-        for h in range(2):
+        for h in range(HALVES):
             nc.vector.quantize_mx(
                 out=hid_w[h][:].bitcast(E5M2), scales=hid_s[h][:], in_=hid[h][:].rearrange("p j t -> p (j t)")
             )
 
-        p_sb = [sb("p_sb%d" % n, [P, J], F32) for n in range(2)]
-        for h in range(2):
-            for n in range(2):
-                p_ps = psum.tile([P, HALF], F32, name="p_ps%d%d" % (h, n), tag="bank%d" % (2 * h + n))
+        p_sb = [sb("p_sb%d" % n, [P, J], F32) for n in range(N_TILES)]
+        for h in range(HALVES):
+            for n in range(N_TILES):
+                features = slice(n * P, (n + 1) * P)
+                p_ps = psum.tile([P, HALF], F32, name="p_ps%d%d" % (h, n), tag="bank%d" % (N_TILES * h + n))
                 nc.tensor.matmul_mx(
-                    out=p_ps[:], lhsT=wb_w[:, n * P : (n + 1) * P].bitcast(E4M3), lhsT_scale=wb_s[:, n * P : (n + 1) * P],
+                    out=p_ps[:], lhsT=wb_w[:, features].bitcast(E4M3), lhsT_scale=wb_s[:, features],
                     rhs=hid_w[h][:].bitcast(E5M2), rhs_scale=hid_s[h][:], start=True, stop=True,
                 )
                 dst = p_sb[n][:, h * HALF : (h + 1) * HALF]
-                if h == 1 and n == 0:
+                if h == HALVES - 1 and n == 0:
                     nc.vector.tensor_copy(dst, p_ps[:])
                 else:
                     nc.scalar.copy(dst, p_ps[:])
 
-        for n in range(2):
+        for n in range(N_TILES):
             nc.vector.memset(pages[n][:], 0.0)
-        ends = [sb("ends%d" % n, [P, U], F32) for n in range(2)]
-        for n in range(2):
+        ends = [sb("ends%d" % n, [P, U], F32) for n in range(N_TILES)]
+        for n in range(N_TILES):
             nc.scalar.activation(ends[n][:], p_sb[n][:].indirect(idx5[:]), ACT.Copy, scale=so_t[:, n : n + 1])
         nc.vector.tensor_copy(pages[0][:].indirect(idx6[:]), ends[0][:])
         nc.scalar.activation(pages[1][:].indirect(idx6[:]), ends[1][:], ACT.Copy)

from contextlib import ExitStack

import concourse.mybir as mybir

K, T, Z, J, R, N, U, E = 512, 1024, 1024, 256, 512, 256, 128, 512
FLOPS = 2 * K * R * J * 4 + 2 * R * N * J

F32 = mybir.dt.float32
BF16 = mybir.dt.bfloat16
I32 = mybir.dt.int32
U32 = mybir.dt.uint32
U16 = mybir.dt.uint16
U8 = mybir.dt.uint8
E4M3 = mybir.dt.float8_e4m3fn_x4
E5M2 = mybir.dt.float8_e5m2_x4
E2M1 = mybir.dt.float4_e2m1fn_x4
ALU = mybir.AluOpType
ACT = mybir.ActivationFunctionType

P = 128
PACK = 4
QUAD = 32
LIVE = 4
HALF_P = P // 2
HALVES = 2
HALF = J // HALVES
HALF_COLS = HALF // 16
N_TILES = N // P
W, W2 = 0, 1


def tile_list_betweenweighed_crossed_one_postedout_kernel(
    tc, xt_words, xt_scales, xo_words, xo_scales, w_words, w_scales, w2_words, w2_scales, sa,
    wb_words, wb_scales, so, offs, offs2, offs3, offs4, offs5, offs6, out,
):
    nc = tc.nc
    with ExitStack() as ctx:
        pool = ctx.enter_context(tc.tile_pool(name="pool", bufs=1))
        psum = ctx.enter_context(tc.psum_pool(name="psum", bufs=1))

        def sb(name, shape, dtype):
            return pool.tile(shape, dtype, name=name, align_bytes=64)

        def load_list(name, src):
            dst = pool.tile(list(src.shape), U16, name=name)
            nc.sync.dma_start(dst[:], src)
            return dst

        def load_words(name, src, width, dtype):
            dst = sb(name, [P, width], dtype)
            nc.sync.dma_start(dst[:].bitcast(I32), src.bitcast(I32))
            return dst

        def load_scale_rows(queues, dst, src):
            rows = src[0].bitcast(I32).rearrange("(u q row) c -> q row u c", u=2, q=2)
            for q, queue in enumerate(queues):
                queue.dma_start(dst[QUAD * q : QUAD * q + LIVE], rows[q])

        xt_rows = sb("xt_rows", [HALF_P, 2, T], U8)
        xo_rows = sb("xo_rows", [HALF_P, 2, Z], U8)
        ww_s = sb("ww_s", [P, 2, 2, R], U8)
        wb_s = sb("wb_s", [P, N], U8)
        ww_view = ww_s[:].bitcast(I32)
        nc.vector.memset(xt_rows[:].bitcast(I32), 0)
        nc.vector.memset(xo_rows[:].bitcast(I32), 0)
        nc.vector.memset(ww_view[HALF_P:P], 0)
        nc.vector.memset(wb_s[:].bitcast(I32), 0)

        idx = load_list("idx", offs)
        xt_w = load_words("xt_w", xt_words[0], T, U16)
        idx2 = load_list("idx2", offs2)
        load_scale_rows((nc.scalar, nc.sync), xt_rows[:].bitcast(I32), xt_scales)
        load_scale_rows((nc.sync, nc.sync), xo_rows[:].bitcast(I32), xo_scales)
        w_raw = load_words("w_raw", w_words[0].rearrange("p c t -> p (c t)"), R, U32)
        xo_w = load_words("xo_w", xo_words[0].rearrange("p c t -> p (c t)"), Z, U32)
        load_scale_rows((nc.sync, nc.sync), ww_view[HALF_P:P, :, W, :], w_scales)
        load_scale_rows((nc.sync, nc.sync), ww_view[HALF_P:P, :, W2, :], w2_scales)
        w2_raw = load_words("w2_raw", w2_words[0].rearrange("p c t -> p (c t)"), R, U32)
        idx3 = load_list("idx3", offs3)
        sa_t = sb("sa_t", [P, PACK], F32)
        nc.sync.dma_start(sa_t[:], sa.rearrange("(p t) o -> p (t o)", t=PACK))
        idx4 = load_list("idx4", offs4)
        idx5 = load_list("idx5", offs5)
        wb_w = load_words("wb_w", wb_words[0].rearrange("p c t -> p (c t)"), N, U32)
        for q in range(P // QUAD):
            nc.sync.dma_start(
                wb_s[QUAD * q : QUAD * q + LIVE].bitcast(I32), wb_scales[0, LIVE * q : LIVE * q + LIVE].bitcast(I32)
            )
        so_t = sb("so_t", [P, N_TILES], F32)
        with nc.allow_non_contiguous_dma(reason="one value of so a partition and output tile"):
            nc.sync.dma_start(so_t[:], so.rearrange("(n p) o -> p (n o)", p=P))
        idx6 = load_list("idx6", offs6)

        xtg_s = sb("xtg_s", [P, J], U8)
        xtg_w = sb("xtg_w", [P, J], U16)
        xog_s = sb("xog_s", [P, J], U8)
        xog_w = sb("xog_w", [P, J], U32)
        xt_s = sb("xt_s", [P, T], U8)
        xo_s = sb("xo_s", [P, Z], U8)
        nc.vector.tensor_copy(xtg_w[:], xt_w[:].indirect(idx[:]))
        for u in range(2):
            for plane, rows in ((xt_s, xt_rows), (xo_s, xo_rows)):
                nc.vector.tensor_copy(plane[HALF_P * u : HALF_P * (u + 1)].bitcast(I32), rows[:, u, :].bitcast(I32))
        nc.vector.tensor_copy(xtg_s[:], xt_s[:].indirect(idx[:]))

        w_w = sb("w_w", [P, PACK, P], U32)
        w2_w = sb("w2_w", [P, PACK, P], U32)
        ww_p = sb("ww_p", [P, PACK, 2, P], U8)
        for dst, src in ((w_w, w_raw), (w2_w, w2_raw)):
            nc.scalar.copy(
                dst[:].rearrange("p (e f) (c i) -> p c e i f", i=4, f=2),
                src[:].rearrange("p (c i e f) -> p c e i f", i=4, e=2, f=2),
            )

        nc.vector.tensor_copy(xog_s[:], xo_s[:].indirect(idx2[:]))
        nc.vector.tensor_copy(xog_w[:], xo_w[:].indirect(idx2[:]))
        nc.vector.tensor_copy(ww_view[0:HALF_P, 1], ww_view[HALF_P:P, 0])
        for t in range(PACK):
            nc.vector.tensor_copy(ww_p[:, t], ww_s[:, 1].rearrange("p s (m t) -> p t s m", t=PACK)[:, t])

        matrices = {W: (w_w, E5M2), W2: (w2_w, E4M3)}
        tokens = (xtg_w, xtg_s, E2M1)
        notes = (xog_w, xog_s, E5M2)

        def product(acc, matrix, t, table, cols, start, stop):
            words, fmt = matrices[matrix]
            x_w, x_s, x_fmt = table
            nc.tensor.matmul_mx(
                out=acc, lhsT=words[:, t, :].bitcast(fmt), lhsT_scale=ww_p[:, t, matrix, :],
                rhs=x_w[:, cols].bitcast(x_fmt), rhs_scale=x_s[:, cols], start=start, stop=stop,
            )

        a_ps = [psum.tile([P, J], F32, name="a_ps%d" % t, tag="bank%d" % t) for t in range(PACK)]
        b_ps = [psum.tile([P, PACK, HALF], F32, name="b_ps%d" % h) for h in range(HALVES)]
        for t in range(PACK):
            product(a_ps[t][:], W, t, tokens, slice(0, J), True, False)
            product(a_ps[t][:], W2, t, notes, slice(0, J), False, True)
        for h in range(HALVES):
            cols = slice(h * HALF, (h + 1) * HALF)
            for t in range(PACK):
                product(b_ps[h][:, t, :], W2, t, tokens, cols, True, False)
                product(b_ps[h][:, t, :], W, t, notes, cols, False, True)

        pages = [sb("page%d" % n, [P, E], F32) for n in range(N_TILES)]
        a_sb = [sb("a_sb%d" % t, [P, J], F32) for t in range(PACK)]
        scaled = [sb("scaled%d" % h, [P, PACK, HALF], F32) for h in range(HALVES)]
        diff = [sb("diff%d" % h, [P, PACK, HALF], F32) for h in range(HALVES)]
        mag = [sb("mag%d" % h, [P, PACK, HALF], F32) for h in range(HALVES)]
        nc.scalar.copy(a_sb[0][:], a_ps[0][:])
        for t in range(1, PACK):
            nc.vector.tensor_copy(a_sb[t][:], a_ps[t][:])
        for h in range(HALVES):
            entries = slice(HALF_COLS * h, HALF_COLS * (h + 1))
            for t in range(PACK):
                nc.scalar.activation(
                    scaled[h][:, t, :], a_sb[t][:].indirect(idx3[:, entries]), ACT.Copy, scale=sa_t[:, t : t + 1]
                )
        for h in range(HALVES):
            entries = slice(HALF_COLS * h, HALF_COLS * (h + 1))
            for t in range(PACK):
                nc.vector.tensor_tensor(
                    diff[h][:, t, :], a_sb[t][:].indirect(idx4[:, entries]), scaled[h][:, t, :], ALU.subtract
                )
            for tiles in (slice(0, PACK - 1), slice(PACK - 1, PACK)):
                nc.scalar.activation(mag[h][:, tiles, :], diff[h][:, tiles, :], ACT.Abs)

        hid = [sb("hid%d" % h, [P, HALF, PACK], BF16) for h in range(HALVES)]
        hid_w = [sb("hid_w%d" % h, [P, HALF], U32) for h in range(HALVES)]
        hid_s = [sb("hid_s%d" % h, [P, HALF], U8) for h in range(HALVES)]
        for h in range(HALVES):
            nc.vector.tensor_tensor(
                hid[h][:].rearrange("p (c i) t -> p c t i", i=2),
                mag[h][:].rearrange("p t (c i) -> p c t i", i=2),
                b_ps[h][:].rearrange("p t (c i) -> p c t i", i=2),
                ALU.max,
            )
        for h in range(HALVES):
            nc.vector.quantize_mx(
                out=hid_w[h][:].bitcast(E5M2), scales=hid_s[h][:], in_=hid[h][:].rearrange("p j t -> p (j t)")
            )

        p_sb = [sb("p_sb%d" % n, [P, J], F32) for n in range(N_TILES)]
        for h in range(HALVES):
            for n in range(N_TILES):
                features = slice(n * P, (n + 1) * P)
                p_ps = psum.tile([P, HALF], F32, name="p_ps%d%d" % (h, n), tag="bank%d" % (N_TILES * h + n))
                nc.tensor.matmul_mx(
                    out=p_ps[:], lhsT=wb_w[:, features].bitcast(E4M3), lhsT_scale=wb_s[:, features],
                    rhs=hid_w[h][:].bitcast(E5M2), rhs_scale=hid_s[h][:], start=True, stop=True,
                )
                dst = p_sb[n][:, h * HALF : (h + 1) * HALF]
                if h == HALVES - 1 and n == 0:
                    nc.vector.tensor_copy(dst, p_ps[:])
                else:
                    nc.scalar.copy(dst, p_ps[:])

        for n in range(N_TILES):
            nc.vector.memset(pages[n][:], 0.0)
        ends = [sb("ends%d" % n, [P, U], F32) for n in range(N_TILES)]
        for n in range(N_TILES):
            nc.scalar.activation(ends[n][:], p_sb[n][:].indirect(idx5[:]), ACT.Copy, scale=so_t[:, n : n + 1])
        nc.vector.tensor_copy(pages[0][:].indirect(idx6[:]), ends[0][:])
        nc.scalar.activation(pages[1][:].indirect(idx6[:]), ends[1][:], ACT.Copy)
        nc.sync.dma_start(out[0:P, :], pages[0][:])
        nc.scalar.dma_start(out[P : 2 * P, :], pages[1][:])
